import numpy as np, ml_dtypes
CORES = [2,6,26,30,66,70,74,78,82,86]
N = 10
import mx_ref
NC, G = 128, 4
C = np.float32(0.029)
BF = ml_dtypes.bfloat16
def cut(t, i, w=512):
    return t[:, w * i:w * i + w]
def tile(rs):
    return np.stack(rs, axis=2).reshape(128, -1).astype(BF)
def layer(w, X):
    out = []
    for i in range(G):
        for t in range(len(X)):
            p = mx_ref.matmul(mx_ref.quantize(cut(w, len(X) * i + t)), X[t])
            z = p if t == 0 else z + p
        out.append(z)
    return out
def setup_inputs(rng):
    def f(*shape):
        return mx_ref.flush((rng.standard_normal(shape, dtype=np.float32) * np.exp2(rng.integers(-2, 3, shape[:-1] + (1,)))).astype(BF))
    return {"x": f(N, 128, 4 * NC), "w": f(N, 128, 512), "a": np.broadcast_to(f(1, 128, 4 * 512), (N, 128, 4 * 512)).copy(), "bb": f(N, 128, 512)}
def setup_inputs_blocks(rng):
    d = setup_inputs(rng)
    for k in ("x", "w", "bb"): d[k] = mx_ref.spread(d[k], rng, 4)
    return d
def setup_inputs_wide(rng):
    d = setup_inputs(rng)
    for k in ("x", "w", "bb"): d[k] = mx_ref.flush((d[k].astype(np.float32) * np.exp2(rng.integers(-6, 7, (N, 1, 1))).astype(np.float32)).astype(BF))
    return d
def setup_inputs_zeros(rng):
    d = setup_inputs(rng); v = d["x"].reshape(N, 128, -1, 4).copy()
    v[np.broadcast_to((rng.random((N, 1, v.shape[2], 1)) < 0.33), v.shape)] = 0
    d["x"] = v.reshape(d["x"].shape)
    return d
def reference(x, w, a, bb):
    X = [mx_ref.quantize(x[j]) for j in range(N)]
    T = [mx_ref.quantize(tile([z * C for z in layer(a[j], [X[j]])])) for j in range(N)]
    y = np.zeros((N, 128, N * NC), np.float32)
    for r in range(N):
        qw = mx_ref.quantize(w[r]); qb = mx_ref.quantize(bb[r])
        for j in range(N):
            y[r][:, NC * j:NC * j + NC] = mx_ref.matmul(qw, X[j]) + mx_ref.matmul(qb, T[j])
    return {"y": y}

@@ -1,0 +1,237 @@
+import numpy as np
+from concourse.bass import DstId, RemoteDMATransfer
+from concourse.mybir import dt, AluOpType, ActivationFunctionType
+
+NC = 128
+SLOTS = 10
+GROUPS = [(0, 2), (2, 2), (4, 2), (6, 2), (8, 1), (9, 1)]
+C = float(np.float32(0.029))
+
+SCRATCH = {
+    "bx": ("sbuf", [128, 512], "bfloat16"),
+    "ba": ("sbuf", [128, 2048], "bfloat16"),
+    "bw": ("sbuf", [128, 1024], "bfloat16"),
+    "qx": ("sbuf", [128, NC * SLOTS], "float8_e4m3fn_x4"),
+    "sx": ("sbuf", [128, NC * SLOTS], "uint8"),
+    "qa": ("sbuf", [128, 512], "float8_e4m3fn_x4"),
+    "sa": ("sbuf", [128, 512], "uint8"),
+    "qw": ("sbuf", [128, 256], "float8_e4m3fn_x4"),
+    "sw": ("sbuf", [128, 256], "uint8"),
+    "h": ("sbuf", [128, 4 * NC * SLOTS], "bfloat16"),
+    "qt": ("sbuf", [128, NC * SLOTS], "float8_e4m3fn_x4"),
+    "st": ("sbuf", [128, NC * SLOTS], "uint8"),
+    "ys": ("sbuf", [128, NC * SLOTS], "float32"),
+    "z": ("psum", [128, 2048], "float32"),
+    "yp": ("psum", [128, 2048], "float32"),
+}
+SEMAPHORES = (["lx", "la", "lw", "xq", "aq", "wq", "sent", "sd", "own"]
+              + ["c%d" % i for i in range(10)] + ["f%d" % i for i in range(4)]
+              + ["zs", "ss", "vs", "qs", "yd", "es", "stored"])
+
+
+def _path(topo, a, b):
+    if topo.mates(a, b):
+        return [("mate", a)]
+    if topo.same_plane(a, b):
+        return [("out", a), ("in", b)]
+    m = [c for c in range(topo.CHIPS) if topo.mates(a, c)][0]
+    return [("mate", a), ("out", m), ("in", b)]
+
+
+def _perms(items):
+    if not items:
+        return [[]]
+    return [[x] + p for i, x in enumerate(items) for p in _perms(items[:i] + items[i + 1:])]
+
+
+def _ring(topo, chips):
+    best = None
+    n = len(chips)
+    for p in _perms(chips[1:]):
+        order = [chips[0]] + p
+        cost = 0
+        for k in range(1, n):
+            use = {}
+            for i in range(n):
+                for l in _path(topo, order[i], order[(i + k) % n]):
+                    use[l] = use.get(l, 0) + 1
+            cost += sum(u - 1 for u in use.values())
+        if best is None or cost < best[0]:
+            best = (cost, order)
+    return best[1]
+
+
+def _bits(mask):
+    return [1 << i for i in range(mask.bit_length()) if mask >> i & 1]
+
+
+def rank_program(g, core, T, topo):
+    rank = T.rank_of(core)
+    if rank is None:
+        return
+    S = T.sem
+    cores = list(T.cores)
+    chips = []
+    for c in cores:
+        if topo.chip(c) not in chips:
+            chips.append(topo.chip(c))
+    ring = _ring(topo, chips)
+    n = len(ring)
+    me = ring.index(topo.chip(core))
+    mate = [c for c in cores if topo.chip(c) == topo.chip(core) and c != core][0]
+
+    def twin(chip, die):
+        return [c for c in cores if topo.chip(c) == chip and topo.die(c) == die][0]
+
+    die, odie = topo.die(core), topo.die(mate)
+    dsts = [twin(ring[(me + k) % n], die) for k in range(1, n)]
+    srcs = [twin(ring[(me - k) % n], die) for k in range(1, n)]
+    fsrcs = [twin(ring[(me - k) % n], odie) for k in range(1, n)]
+    pair = sorted([rank, T.rank_of(mate)])
+    slot_rank = pair + [T.rank_of(c) for c in srcs + fsrcs]
+    mine = pair.index(rank)
+    arr = ["c%d" % T.rank_of(c) for c in srcs]
+
+    link = topo.mask(core, dsts[0])
+    for d in dsts:
+        link &= topo.mask(core, d)
+    chipwide = topo.mask(core, mate)
+    inner = chipwide & ~link
+    ib = _bits(inner)
+    half0, half1 = sum(ib[:len(ib) // 2]), sum(ib[len(ib) // 2:])
+    NL, NI, NA = len(_bits(link)), len(ib), len(_bits(chipwide))
+
+    def ident(c):
+        rid, pid, _ = topo.addr(c)
+        return DstId(rid=rid, pnc=pid)
+
+    def codes(s, k=1):
+        return T.qx[:, NC * s:NC * (s + k)].bitcast(dt.uint8)
+
+    def planes(s, k=1):
+        return T.sx[:, NC * s:NC * (s + k)]
+
+    g.sync.dma_start(T.bx[:], T.x[:]).then_inc(S.lx, 16)
+    g.sync.dma_start(T.ba[:], T.a[:]).then_inc(S.la, 16)
+    g.sync.dma_start(T.bw[:, 0:512], T.w[:]).then_inc(S.lw, 16)
+    g.sync.dma_start(T.bw[:, 512:1024], T.bb[:]).then_inc(S.lw, 16)
+
+    sent = [0]
+
+    def fused(transfers, engines):
+        g.remote_dma_fused(transfers, local_sem=S.sent)
+        sent[0] += engines
+
+    def one(dst, src, sem, mask):
+        rid, pid, _ = topo.addr(mate)
+        g.remote_dma(dst, src, sem, S.sent, pid, rid, mask)
+        sent[0] += len(_bits(mask))
+
+    g.wait_ge(S.xq, 1)
+    ids = [ident(d) for d in dsts]
+    fused([RemoteDMATransfer(dst_ids=ids, dma_engine_mask=link, remote_sem=S.sd, srcs=[planes(mine)],
+                             dsts=[planes(2 + k) for k in range(n - 1)])], NL)
+    fused([RemoteDMATransfer(dst_ids=ids, dma_engine_mask=link, remote_sem=S["c%d" % rank], srcs=[codes(mine)],
+                             dsts=[codes(2 + k) for k in range(n - 1)])], NL)
+    one(planes(mine), planes(mine), S.own, inner)
+    one(codes(mine), codes(mine), S.own, inner)
+    g.wait_ge(S.sd, NL * (n - 1))
+    g.wait_ge(S[arr[0]], NL)
+    fused([RemoteDMATransfer(dst_ids=[ident(mate)], dma_engine_mask=half0, remote_sem=S.f0, srcs=[codes(2)],
+                             dsts=[codes(6)]),
+           RemoteDMATransfer(dst_ids=[ident(mate)], dma_engine_mask=half1, remote_sem=S.f0, srcs=[planes(2, 4)],
+                             dsts=[planes(6, 4)])], NI)
+    for k in (1, 2, 3):
+        g.wait_ge(S[arr[k]], NL)
+        one(codes(6 + k), codes(2 + k), S["f%d" % k], inner if k < 3 else chipwide)
+    g.wait_ge(S.sent, sent[0])
+
+    need = {mine: [(S.xq, 1)], 1 - mine: [(S.own, 2 * NI)],
+            2: [(S.sd, NL * (n - 1)), (S[arr[0]], NL)], 6: [(S.f0, NI)], 9: [(S.f3, NA)]}
+    for k in (1, 2, 3):
+        need[2 + k] = [(S[arr[k]], NL)]
+    for k in (1, 2):
+        need[6 + k] = [(S["f%d" % k], NI)]
+
+    def cols(k):
+        s, m = GROUPS[k]
+        return NC * s, NC * m
+
+    def bt(k):
+        a, w = cols(k)
+        y0 = 512 * (k % 4)
+        g.tensor.wait_ge(S.qs, k + 1)
+        g.tensor.matmul_mx(T.yp[:, y0:y0 + w], T.qw[:, 128:256], T.sw[:, 128:256],
+                           T.qt[:, a:a + w], T.st[:, a:a + w], False, True).then_inc(S.yd, 1)
+
+    for k in range(len(GROUPS)):
+        a, w = cols(k)
+        if k == 0:
+            g.tensor.wait_ge(S.aq, 1)
+        for s in range(GROUPS[k][0], GROUPS[k][0] + GROUPS[k][1]):
+            for sem, v in need[s]:
+                g.tensor.wait_ge(sem, v)
+        for b in range(4):
+            if k > 0:
+                g.tensor.wait_ge(S.vs if b % 2 else S.ss, 2 * (k - 1) + b // 2 + 1)
+            g.tensor.matmul_mx(T.z[:, 512 * b:512 * b + w], T.qa[:, NC * b:NC * b + NC], T.sa[:, NC * b:NC * b + NC],
+                               T.qx[:, a:a + w], T.sx[:, a:a + w], True, True).then_inc(S.zs, 1)
+        if k == 0:
+            g.tensor.wait_ge(S.wq, 1)
+        if k >= 4:
+            g.tensor.wait_ge(S.es, k - 3)
+        y0 = 512 * (k % 4)
+        g.tensor.matmul_mx(T.yp[:, y0:y0 + w], T.qw[:, 0:128], T.sw[:, 0:128],
+                           T.qx[:, a:a + w], T.sx[:, a:a + w], True, False)
+        if k > 0:
+            bt(k - 1)
+    bt(len(GROUPS) - 1)
+
+    def out(k):
+        a, w = cols(k)
+        y0 = 512 * (k % 4)
+        g.scalar.wait_ge(S.yd, k + 1)
+        g.scalar.activation(T.ys[:, a:a + w], T.yp[:, y0:y0 + w], ActivationFunctionType.Copy).then_inc(S.es, 1)
+
+    for k in range(len(GROUPS)):
+        a, w = cols(k)
+        for b in (0, 2):
+            g.scalar.wait_ge(S.zs, 4 * k + b + 1)
+            g.scalar.activation(T.h[:, 4 * a + b:4 * (a + w):4], T.z[:, 512 * b:512 * b + w],
+                                ActivationFunctionType.Copy, scale=C).then_inc(S.ss, 1)
+        if k > 0:
+            out(k - 1)
+    out(len(GROUPS) - 1)
+
+    g.vector.wait_ge(S.lx, 16)
+    g.vector.quantize_mx(T.qx[:, NC * mine:NC * mine + NC], T.sx[:, NC * mine:NC * mine + NC],
+                         T.bx[:]).then_inc(S.xq, 1)
+    g.vector.wait_ge(S.la, 16)
+    g.vector.quantize_mx(T.qa[:], T.sa[:], T.ba[:]).then_inc(S.aq, 1)
+    g.vector.wait_ge(S.lw, 32)
+    g.vector.quantize_mx(T.qw[:], T.sw[:], T.bw[:]).then_inc(S.wq, 1)
+    for k in range(len(GROUPS)):
+        a, w = cols(k)
+        for b in (1, 3):
+            g.vector.wait_ge(S.zs, 4 * k + b + 1)
+            g.vector.tensor_scalar(T.h[:, 4 * a + b:4 * (a + w):4], T.z[:, 512 * b:512 * b + w],
+                                   C, None, AluOpType.mult).then_inc(S.vs, 1)
+        g.vector.wait_ge(S.vs, 2 * k + 2)
+        g.vector.wait_ge(S.ss, 2 * k + 2)
+        g.vector.quantize_mx(T.qt[:, a:a + w], T.st[:, a:a + w], T.h[:, 4 * a:4 * (a + w)]).then_inc(S.qs, 1)
+
+    stores = [0]
+    for k in range(len(GROUPS)):
+        g.sync.wait_ge(S.es, k + 1)
+        s0, m = GROUPS[k]
+        runs = [[s0, 1]]
+        for s in range(s0 + 1, s0 + m):
+            if slot_rank[s] == slot_rank[s - 1] + 1:
+                runs[-1][1] += 1
+            else:
+                runs.append([s, 1])
+        for s, m2 in runs:
+            j = slot_rank[s]
+            g.sync.dma_start(T.y[:, NC * j:NC * (j + m2)], T.ys[:, NC * s:NC * (s + m2)]).then_inc(S.stored, 16)
+            stores[0] += 16
+    g.sync.wait_ge(S.stored, stores[0])

@@ -4,7 +4,15 @@ from concourse.mybir import dt, AluOpType, ActivationFunctionType
 
 NC = 128
 SLOTS = 10
-GROUPS = [(0, 2), (2, 2), (4, 2), (6, 2), (8, 1), (9, 1)]
+GR = {"A": (2, 2), "B": (4, 2), "C": (6, 2), "D": (8, 1), "E": (9, 1)}
+MADE = ["O", "P", "A", "B", "D", "E"]
+YBANK = {"O": 0, "P": 1, "A": 2, "B": 3, "D": 0, "C": 1, "E": 2}
+BEFORE = {"D": "O", "C": "P", "E": "A"}
+TENSOR = ["ZO", "WO", "TO", "ZP", "WP", "ZA", "WA", "TP", "ZB", "WB", "TA", "ZD", "WD", "TB", "ZE", "WC", "WE", "TD",
+          "TC", "TE"]
+SCALAR = ["SO", "YO", "SP", "SA", "YP", "SB", "YA", "SD", "YB", "SE", "YD", "YC", "YE"]
+VECTOR = ["SO", "QO", "SP", "QP", "SA", "QA", "SB", "QB", "SD", "QD", "SE", "QE"]
+STORE = ["O", "P", "A", "B", "D", "C", "E"]
 C = float(np.float32(0.029))
 
 SCRATCH = {
@@ -24,9 +32,9 @@ SCRATCH = {
     "z": ("psum", [128, 2048], "float32"),
     "yp": ("psum", [128, 2048], "float32"),
 }
-SEMAPHORES = (["lx", "la", "lw", "xq", "aq", "wq", "sent", "sd", "own"]
-              + ["c%d" % i for i in range(10)] + ["f%d" % i for i in range(4)]
-              + ["zs", "ss", "vs", "qs", "yd", "es", "stored"])
+SEMAPHORES = (["lx", "la", "lw", "xq", "aq", "wq", "sent", "sd0", "sd1", "own", "fp0", "fp1", "fa", "f2", "f3", "ft"]
+              + ["c%d" % i for i in range(10)] + ["zs", "ss", "vs", "stored"]
+              + [p + k for p in "qye" for k in YBANK])
 
 
 def _path(topo, a, b):
@@ -91,25 +99,24 @@ def rank_program(g, core, T, topo):
     slot_rank = pair + [T.rank_of(c) for c in srcs + fsrcs]
     mine = pair.index(rank)
     arr = ["c%d" % T.rank_of(c) for c in srcs]
+    grp = dict(GR, O=(mine, 1), P=(1 - mine, 1))
 
     link = topo.mask(core, dsts[0])
     for d in dsts:
         link &= topo.mask(core, d)
     chipwide = topo.mask(core, mate)
     inner = chipwide & ~link
-    ib = _bits(inner)
-    half0, half1 = sum(ib[:len(ib) // 2]), sum(ib[len(ib) // 2:])
-    NL, NI, NA = len(_bits(link)), len(ib), len(_bits(chipwide))
+    NL, NI, NA = len(_bits(link)), len(_bits(inner)), len(_bits(chipwide))
 
     def ident(c):
         rid, pid, _ = topo.addr(c)
         return DstId(rid=rid, pnc=pid)
 
-    def codes(s, k=1):
-        return T.qx[:, NC * s:NC * (s + k)].bitcast(dt.uint8)
+    def codes(s, k=1, buf="qx"):
+        return T[buf][:, NC * s:NC * (s + k)].bitcast(dt.uint8)
 
-    def planes(s, k=1):
-        return T.sx[:, NC * s:NC * (s + k)]
+    def planes(s, k=1, buf="sx"):
+        return T[buf][:, NC * s:NC * (s + k)]
 
     g.sync.dma_start(T.bx[:], T.x[:]).then_inc(S.lx, 16)
     g.sync.dma_start(T.ba[:], T.a[:]).then_inc(S.la, 16)
@@ -118,120 +125,118 @@ def rank_program(g, core, T, topo):
 
     sent = [0]
 
-    def fused(transfers, engines):
-        g.remote_dma_fused(transfers, local_sem=S.sent)
-        sent[0] += engines
+    def spread(view, steps, sem):
+        g.remote_dma_fused([RemoteDMATransfer(dst_ids=[ident(dsts[k]) for k in steps], dma_engine_mask=link,
+                                              remote_sem=sem, srcs=[view(mine)], dsts=[view(2 + k) for k in steps])],
+                           local_sem=S.sent)
+        sent[0] += NL
 
-    def one(dst, src, sem, mask):
+    def hand(dst, src, sem, mask):
         rid, pid, _ = topo.addr(mate)
         g.remote_dma(dst, src, sem, S.sent, pid, rid, mask)
         sent[0] += len(_bits(mask))
 
     g.wait_ge(S.xq, 1)
-    ids = [ident(d) for d in dsts]
-    fused([RemoteDMATransfer(dst_ids=ids, dma_engine_mask=link, remote_sem=S.sd, srcs=[planes(mine)],
-                             dsts=[planes(2 + k) for k in range(n - 1)])], NL)
-    fused([RemoteDMATransfer(dst_ids=ids, dma_engine_mask=link, remote_sem=S["c%d" % rank], srcs=[codes(mine)],
-                             dsts=[codes(2 + k) for k in range(n - 1)])], NL)
-    one(planes(mine), planes(mine), S.own, inner)
-    one(codes(mine), codes(mine), S.own, inner)
-    g.wait_ge(S.sd, NL * (n - 1))
+    for steps, sem in (((0, 1), S.sd0), ((2, 3), S.sd1)):
+        spread(planes, steps, sem)
+        spread(codes, steps, S["c%d" % rank])
+    hand(planes(mine), planes(mine), S.own, inner)
+    hand(codes(mine), codes(mine), S.own, inner)
+    g.wait_ge(S.sd0, 2 * NL)
+    hand(planes(6, 2), planes(2, 2), S.fp0, inner)
     g.wait_ge(S[arr[0]], NL)
-    fused([RemoteDMATransfer(dst_ids=[ident(mate)], dma_engine_mask=half0, remote_sem=S.f0, srcs=[codes(2)],
-                             dsts=[codes(6)]),
-           RemoteDMATransfer(dst_ids=[ident(mate)], dma_engine_mask=half1, remote_sem=S.f0, srcs=[planes(2, 4)],
-                             dsts=[planes(6, 4)])], NI)
-    for k in (1, 2, 3):
-        g.wait_ge(S[arr[k]], NL)
-        one(codes(6 + k), codes(2 + k), S["f%d" % k], inner if k < 3 else chipwide)
+    g.wait_ge(S[arr[1]], NL)
+    hand(codes(6, 2), codes(2, 2), S.fa, inner)
+    g.wait_ge(S.sd1, 2 * NL)
+    hand(planes(8, 2), planes(4, 2), S.fp1, inner)
+    g.wait_ge(S[arr[2]], NL)
+    hand(codes(8), codes(4), S.f2, inner)
+    g.wait_ge(S[arr[3]], NL)
+    hand(codes(9), codes(5), S.f3, chipwide)
+    g.wait_ge(S.qA, 1)
+    hand(planes(6, 2, "st"), planes(2, 2, "st"), S.ft, chipwide)
+    hand(codes(6, 2, "qt"), codes(2, 2, "qt"), S.ft, chipwide)
     g.wait_ge(S.sent, sent[0])
 
-    need = {mine: [(S.xq, 1)], 1 - mine: [(S.own, 2 * NI)],
-            2: [(S.sd, NL * (n - 1)), (S[arr[0]], NL)], 6: [(S.f0, NI)], 9: [(S.f3, NA)]}
-    for k in (1, 2, 3):
-        need[2 + k] = [(S[arr[k]], NL)]
-    for k in (1, 2):
-        need[6 + k] = [(S["f%d" % k], NI)]
+    need = {"O": [(S.xq, 1)],
+            "P": [(S.own, 2 * NI)],
+            "A": [(S.sd0, 2 * NL), (S[arr[0]], NL), (S[arr[1]], NL)],
+            "B": [(S.sd1, 2 * NL), (S[arr[2]], NL), (S[arr[3]], NL)],
+            "C": [(S.fp0, NI), (S.fa, NI)],
+            "D": [(S.fp1, NI), (S.f2, NI)],
+            "E": [(S.f3, NA)]}
 
     def cols(k):
-        s, m = GROUPS[k]
-        return NC * s, NC * m
+        return slice(NC * grp[k][0], NC * (grp[k][0] + grp[k][1]))
 
-    def bt(k):
-        a, w = cols(k)
-        y0 = 512 * (k % 4)
-        g.tensor.wait_ge(S.qs, k + 1)
-        g.tensor.matmul_mx(T.yp[:, y0:y0 + w], T.qw[:, 128:256], T.sw[:, 128:256],
-                           T.qt[:, a:a + w], T.st[:, a:a + w], False, True).then_inc(S.yd, 1)
+    def zbank(k, b):
+        return T.z[:, 512 * b:512 * b + NC * grp[k][1]]
 
-    for k in range(len(GROUPS)):
-        a, w = cols(k)
-        if k == 0:
-            g.tensor.wait_ge(S.aq, 1)
-        for s in range(GROUPS[k][0], GROUPS[k][0] + GROUPS[k][1]):
-            for sem, v in need[s]:
+    def ybank(k):
+        return T.yp[:, 512 * YBANK[k]:512 * YBANK[k] + NC * grp[k][1]]
+
+    seen = []
+    for op in TENSOR:
+        k = op[1]
+        if op[0] in "ZW" and k not in seen:
+            if not seen:
+                g.tensor.wait_ge(S.aq, 1)
+            seen.append(k)
+            for sem, v in need[k]:
                 g.tensor.wait_ge(sem, v)
-        for b in range(4):
-            if k > 0:
-                g.tensor.wait_ge(S.vs if b % 2 else S.ss, 2 * (k - 1) + b // 2 + 1)
-            g.tensor.matmul_mx(T.z[:, 512 * b:512 * b + w], T.qa[:, NC * b:NC * b + NC], T.sa[:, NC * b:NC * b + NC],
-                               T.qx[:, a:a + w], T.sx[:, a:a + w], True, True).then_inc(S.zs, 1)
-        if k == 0:
-            g.tensor.wait_ge(S.wq, 1)
-        if k >= 4:
-            g.tensor.wait_ge(S.es, k - 3)
-        y0 = 512 * (k % 4)
-        g.tensor.matmul_mx(T.yp[:, y0:y0 + w], T.qw[:, 0:128], T.sw[:, 0:128],
-                           T.qx[:, a:a + w], T.sx[:, a:a + w], True, False)
-        if k > 0:
-            bt(k - 1)
-    bt(len(GROUPS) - 1)
-
-    def out(k):
-        a, w = cols(k)
-        y0 = 512 * (k % 4)
-        g.scalar.wait_ge(S.yd, k + 1)
-        g.scalar.activation(T.ys[:, a:a + w], T.yp[:, y0:y0 + w], ActivationFunctionType.Copy).then_inc(S.es, 1)
-
-    for k in range(len(GROUPS)):
-        a, w = cols(k)
-        for b in (0, 2):
-            g.scalar.wait_ge(S.zs, 4 * k + b + 1)
-            g.scalar.activation(T.h[:, 4 * a + b:4 * (a + w):4], T.z[:, 512 * b:512 * b + w],
-                                ActivationFunctionType.Copy, scale=C).then_inc(S.ss, 1)
-        if k > 0:
-            out(k - 1)
-    out(len(GROUPS) - 1)
+        if op[0] == "Z":
+            i = MADE.index(k)
+            for b in range(4):
+                if i:
+                    g.tensor.wait_ge(S.vs if b % 2 else S.ss, 2 * (i - 1) + b // 2 + 1)
+                g.tensor.matmul_mx(zbank(k, b), T.qa[:, NC * b:NC * b + NC], T.sa[:, NC * b:NC * b + NC],
+                                   T.qx[:, cols(k)], T.sx[:, cols(k)], True, True).then_inc(S.zs, 1)
+        elif op[0] == "W":
+            if len(seen) == 1:
+                g.tensor.wait_ge(S.wq, 1)
+            if k in BEFORE:
+                g.tensor.wait_ge(S["e" + BEFORE[k]], 1)
+            g.tensor.matmul_mx(ybank(k), T.qw[:, 0:128], T.sw[:, 0:128], T.qx[:, cols(k)], T.sx[:, cols(k)], True, False)
+        else:
+            if k in MADE:
+                g.tensor.wait_ge(S["q" + k], 1)
+            else:
+                g.tensor.wait_ge(S.ft, 2 * NA)
+            g.tensor.matmul_mx(ybank(k), T.qw[:, 128:256], T.sw[:, 128:256], T.qt[:, cols(k)], T.st[:, cols(k)],
+                               False, True).then_inc(S["y" + k], 1)
 
     g.vector.wait_ge(S.lx, 16)
-    g.vector.quantize_mx(T.qx[:, NC * mine:NC * mine + NC], T.sx[:, NC * mine:NC * mine + NC],
-                         T.bx[:]).then_inc(S.xq, 1)
+    g.vector.quantize_mx(T.qx[:, cols("O")], T.sx[:, cols("O")], T.bx[:]).then_inc(S.xq, 1)
     g.vector.wait_ge(S.la, 16)
     g.vector.quantize_mx(T.qa[:], T.sa[:], T.ba[:]).then_inc(S.aq, 1)
     g.vector.wait_ge(S.lw, 32)
     g.vector.quantize_mx(T.qw[:], T.sw[:], T.bw[:]).then_inc(S.wq, 1)
-    for k in range(len(GROUPS)):
-        a, w = cols(k)
-        for b in (1, 3):
-            g.vector.wait_ge(S.zs, 4 * k + b + 1)
-            g.vector.tensor_scalar(T.h[:, 4 * a + b:4 * (a + w):4], T.z[:, 512 * b:512 * b + w],
-                                   C, None, AluOpType.mult).then_inc(S.vs, 1)
-        g.vector.wait_ge(S.vs, 2 * k + 2)
-        g.vector.wait_ge(S.ss, 2 * k + 2)
-        g.vector.quantize_mx(T.qt[:, a:a + w], T.st[:, a:a + w], T.h[:, 4 * a:4 * (a + w)]).then_inc(S.qs, 1)
-
-    stores = [0]
-    for k in range(len(GROUPS)):
-        g.sync.wait_ge(S.es, k + 1)
-        s0, m = GROUPS[k]
-        runs = [[s0, 1]]
-        for s in range(s0 + 1, s0 + m):
-            if slot_rank[s] == slot_rank[s - 1] + 1:
-                runs[-1][1] += 1
+    for queue, ops in (("s", SCALAR), ("v", VECTOR)):
+        e = g.scalar if queue == "s" else g.vector
+        for op in ops:
+            k = op[1]
+            lo, hi = 4 * NC * grp[k][0], 4 * NC * (grp[k][0] + grp[k][1])
+            if op[0] == "S":
+                i = MADE.index(k)
+                for b in ((0, 2) if queue == "s" else (1, 3)):
+                    e.wait_ge(S.zs, 4 * i + b + 1)
+                    dst, src = T.h[:, lo + b:hi:4], zbank(k, b)
+                    if queue == "s":
+                        e.activation(dst, src, ActivationFunctionType.Copy, scale=C).then_inc(S.ss, 1)
+                    else:
+                        e.tensor_scalar(dst, src, C, None, AluOpType.mult).then_inc(S.vs, 1)
+            elif op[0] == "Q":
+                i = MADE.index(k)
+                e.wait_ge(S.vs, 2 * i + 2)
+                e.wait_ge(S.ss, 2 * i + 2)
+                e.quantize_mx(T.qt[:, cols(k)], T.st[:, cols(k)], T.h[:, lo:hi]).then_inc(S["q" + k], 1)
             else:
-                runs.append([s, 1])
-        for s, m2 in runs:
+                e.wait_ge(S["y" + k], 1)
+                e.activation(T.ys[:, cols(k)], ybank(k), ActivationFunctionType.Copy).then_inc(S["e" + k], 1)
+
+    for k in STORE:
+        g.sync.wait_ge(S["e" + k], 1)
+        for s in range(grp[k][0], grp[k][0] + grp[k][1]):
             j = slot_rank[s]
-            g.sync.dma_start(T.y[:, NC * j:NC * (j + m2)], T.ys[:, NC * s:NC * (s + m2)]).then_inc(S.stored, 16)
-            stores[0] += 16
-    g.sync.wait_ge(S.stored, stores[0])
+            g.sync.dma_start(T.y[:, NC * j:NC * j + NC], T.ys[:, NC * s:NC * s + NC]).then_inc(S.stored, 16)
+    g.sync.wait_ge(S.stored, 16 * SLOTS)

@@ -4,15 +4,16 @@ from concourse.mybir import dt, AluOpType, ActivationFunctionType
 
 NC = 128
 SLOTS = 10
-GR = {"A": (2, 2), "B": (4, 2), "C": (6, 2), "D": (8, 1), "E": (9, 1)}
-MADE = ["O", "P", "A", "B", "D", "E"]
-YBANK = {"O": 0, "P": 1, "A": 2, "B": 3, "D": 0, "C": 1, "E": 2}
-BEFORE = {"D": "O", "C": "P", "E": "A"}
-TENSOR = ["ZO", "WO", "TO", "ZP", "WP", "ZA", "WA", "TP", "ZB", "WB", "TA", "ZD", "WD", "TB", "ZE", "WC", "WE", "TD",
-          "TC", "TE"]
-SCALAR = ["SO", "YO", "SP", "SA", "YP", "SB", "YA", "SD", "YB", "SE", "YD", "YC", "YE"]
-VECTOR = ["SO", "QO", "SP", "QP", "SA", "QA", "SB", "QB", "SD", "QD", "SE", "QE"]
-STORE = ["O", "P", "A", "B", "D", "C", "E"]
+GR = {"A": (2, 2), "F": (4, 1), "G": (5, 1), "C": (6, 2), "D": (8, 1), "E": (9, 1)}
+MADE = ["O", "P", "A", "F", "G", "E"]
+GIVEN = [("C", "A"), ("D", "F")]
+YBANK = {"O": 0, "P": 1, "A": 2, "F": 3, "G": 0, "D": 1, "E": 2, "C": 3}
+BEFORE = {"G": "O", "D": "P", "E": "A", "C": "F"}
+TENSOR = ["ZO", "WO", "TO", "ZP", "WP", "ZA", "WA", "TP", "ZF", "WF", "TA", "ZG", "WG", "TF", "ZE", "WE", "TG", "WC",
+          "TC", "TE", "WD", "TD"]
+SCALAR = ["SO", "YO", "SP", "SA", "YP", "SF", "YA", "SG", "YF", "SE", "YG", "YC", "YD"]
+VECTOR = ["SO", "QO", "SP", "QP", "SA", "QA", "SF", "QF", "SG", "QG", "SE", "QE", "YE"]
+STORE = ["O", "P", "A", "F", "G", "C", "E", "D"]
 C = float(np.float32(0.029))
 
 SCRATCH = {
@@ -32,9 +33,9 @@ SCRATCH = {
     "z": ("psum", [128, 2048], "float32"),
     "yp": ("psum", [128, 2048], "float32"),
 }
-SEMAPHORES = (["lx", "la", "lw", "xq", "aq", "wq", "sent", "sd0", "sd1", "own", "fp0", "fp1", "fa", "f2", "f3", "ft"]
+SEMAPHORES = (["lx", "la", "lw", "xq", "aq", "wq", "sent", "sd0", "sd1", "own", "fp0", "fp1", "fa", "f2", "f3"]
               + ["c%d" % i for i in range(10)] + ["zs", "ss", "vs", "stored"]
-              + [p + k for p in "qye" for k in YBANK])
+              + [p + k for p in "qyet" for k in YBANK])
 
 
 def _path(topo, a, b):
@@ -153,18 +154,21 @@ def rank_program(g, core, T, topo):
     hand(codes(8), codes(4), S.f2, inner)
     g.wait_ge(S[arr[3]], NL)
     hand(codes(9), codes(5), S.f3, chipwide)
-    g.wait_ge(S.qA, 1)
-    hand(planes(6, 2, "st"), planes(2, 2, "st"), S.ft, chipwide)
-    hand(codes(6, 2, "qt"), codes(2, 2, "qt"), S.ft, chipwide)
+    for to, k in GIVEN:
+        (s0, m), d0 = GR[k], GR[to][0]
+        g.wait_ge(S["q" + k], 1)
+        hand(planes(d0, m, "st"), planes(s0, m, "st"), S["t" + to], chipwide)
+        hand(codes(d0, m, "qt"), codes(s0, m, "qt"), S["t" + to], chipwide)
     g.wait_ge(S.sent, sent[0])
 
     need = {"O": [(S.xq, 1)],
             "P": [(S.own, 2 * NI)],
             "A": [(S.sd0, 2 * NL), (S[arr[0]], NL), (S[arr[1]], NL)],
-            "B": [(S.sd1, 2 * NL), (S[arr[2]], NL), (S[arr[3]], NL)],
+            "F": [(S.sd1, 2 * NL), (S[arr[2]], NL)],
+            "G": [(S.sd1, 2 * NL), (S[arr[3]], NL)],
             "C": [(S.fp0, NI), (S.fa, NI)],
             "D": [(S.fp1, NI), (S.f2, NI)],
-            "E": [(S.f3, NA)]}
+            "E": [(S.fp1, NI), (S.f3, NA)]}
 
     def cols(k):
         return slice(NC * grp[k][0], NC * (grp[k][0] + grp[k][1]))
@@ -201,7 +205,7 @@ def rank_program(g, core, T, topo):
             if k in MADE:
                 g.tensor.wait_ge(S["q" + k], 1)
             else:
-                g.tensor.wait_ge(S.ft, 2 * NA)
+                g.tensor.wait_ge(S["t" + k], 2 * NA)
             g.tensor.matmul_mx(ybank(k), T.qw[:, 128:256], T.sw[:, 128:256], T.qt[:, cols(k)], T.st[:, cols(k)],
                                False, True).then_inc(S["y" + k], 1)
 
@@ -232,7 +236,10 @@ def rank_program(g, core, T, topo):
                 e.quantize_mx(T.qt[:, cols(k)], T.st[:, cols(k)], T.h[:, lo:hi]).then_inc(S["q" + k], 1)
             else:
                 e.wait_ge(S["y" + k], 1)
-                e.activation(T.ys[:, cols(k)], ybank(k), ActivationFunctionType.Copy).then_inc(S["e" + k], 1)
+                if queue == "s":
+                    e.activation(T.ys[:, cols(k)], ybank(k), ActivationFunctionType.Copy).then_inc(S["e" + k], 1)
+                else:
+                    e.tensor_copy(T.ys[:, cols(k)], ybank(k)).then_inc(S["e" + k], 1)
 
     for k in STORE:
         g.sync.wait_ge(S["e" + k], 1)

import numpy as np
from concourse.bass import DstId, RemoteDMATransfer
from concourse.mybir import dt, AluOpType, ActivationFunctionType

NC = 128
SLOTS = 10
GR = {"A": (2, 2), "F": (4, 1), "G": (5, 1), "C": (6, 2), "D": (8, 1), "E": (9, 1)}
MADE = ["O", "P", "A", "F", "G", "E"]
GIVEN = [("C", "A"), ("D", "F")]
YBANK = {"O": 0, "P": 1, "A": 2, "F": 3, "G": 0, "D": 1, "E": 2, "C": 3}
BEFORE = {"G": "O", "D": "P", "E": "A", "C": "F"}
TENSOR = ["ZO", "WO", "TO", "ZP", "WP", "ZA", "WA", "TP", "ZF", "WF", "TA", "ZG", "WG", "TF", "ZE", "WE", "TG", "WC",
          "TC", "TE", "WD", "TD"]
SCALAR = ["SO", "YO", "SP", "SA", "YP", "SF", "YA", "SG", "YF", "SE", "YG", "YC", "YD"]
VECTOR = ["SO", "QO", "SP", "QP", "SA", "QA", "SF", "QF", "SG", "QG", "SE", "QE", "YE"]
STORE = ["O", "P", "A", "F", "G", "C", "E", "D"]
C = float(np.float32(0.029))

SCRATCH = {
    "bx": ("sbuf", [128, 512], "bfloat16"),
    "ba": ("sbuf", [128, 2048], "bfloat16"),
    "bw": ("sbuf", [128, 1024], "bfloat16"),
    "qx": ("sbuf", [128, NC * SLOTS], "float8_e4m3fn_x4"),
    "sx": ("sbuf", [128, NC * SLOTS], "uint8"),
    "qa": ("sbuf", [128, 512], "float8_e4m3fn_x4"),
    "sa": ("sbuf", [128, 512], "uint8"),
    "qw": ("sbuf", [128, 256], "float8_e4m3fn_x4"),
    "sw": ("sbuf", [128, 256], "uint8"),
    "h": ("sbuf", [128, 4 * NC * SLOTS], "bfloat16"),
    "qt": ("sbuf", [128, NC * SLOTS], "float8_e4m3fn_x4"),
    "st": ("sbuf", [128, NC * SLOTS], "uint8"),
    "ys": ("sbuf", [128, NC * SLOTS], "float32"),
    "z": ("psum", [128, 2048], "float32"),
    "yp": ("psum", [128, 2048], "float32"),
}
SEMAPHORES = (["lx", "la", "lw", "xq", "aq", "wq", "sent", "sd0", "sd1", "own", "fp0", "fp1", "fa", "f2", "f3"]
              + ["c%d" % i for i in range(10)] + ["zs", "ss", "vs", "stored"]
              + [p + k for p in "qyet" for k in YBANK])


def _path(topo, a, b):
    if topo.mates(a, b):
        return [("mate", a)]
    if topo.same_plane(a, b):
        return [("out", a), ("in", b)]
    m = [c for c in range(topo.CHIPS) if topo.mates(a, c)][0]
    return [("mate", a), ("out", m), ("in", b)]


def _perms(items):
    if not items:
        return [[]]
    return [[x] + p for i, x in enumerate(items) for p in _perms(items[:i] + items[i + 1:])]


def _ring(topo, chips):
    best = None
    n = len(chips)
    for p in _perms(chips[1:]):
        order = [chips[0]] + p
        cost = 0
        for k in range(1, n):
            use = {}
            for i in range(n):
                for l in _path(topo, order[i], order[(i + k) % n]):
                    use[l] = use.get(l, 0) + 1
            cost += sum(u - 1 for u in use.values())
        if best is None or cost < best[0]:
            best = (cost, order)
    return best[1]


def _bits(mask):
    return [1 << i for i in range(mask.bit_length()) if mask >> i & 1]


def rank_program(g, core, T, topo):
    rank = T.rank_of(core)
    if rank is None:
        return
    S = T.sem
    cores = list(T.cores)
    chips = []
    for c in cores:
        if topo.chip(c) not in chips:
            chips.append(topo.chip(c))
    ring = _ring(topo, chips)
    n = len(ring)
    me = ring.index(topo.chip(core))
    mate = [c for c in cores if topo.chip(c) == topo.chip(core) and c != core][0]

    def twin(chip, die):
        return [c for c in cores if topo.chip(c) == chip and topo.die(c) == die][0]

    die, odie = topo.die(core), topo.die(mate)
    dsts = [twin(ring[(me + k) % n], die) for k in range(1, n)]
    srcs = [twin(ring[(me - k) % n], die) for k in range(1, n)]
    fsrcs = [twin(ring[(me - k) % n], odie) for k in range(1, n)]
    pair = sorted([rank, T.rank_of(mate)])
    slot_rank = pair + [T.rank_of(c) for c in srcs + fsrcs]
    mine = pair.index(rank)
    arr = ["c%d" % T.rank_of(c) for c in srcs]
    grp = dict(GR, O=(mine, 1), P=(1 - mine, 1))

    link = topo.mask(core, dsts[0])
    for d in dsts:
        link &= topo.mask(core, d)
    chipwide = topo.mask(core, mate)
    inner = chipwide & ~link
    NL, NI, NA = len(_bits(link)), len(_bits(inner)), len(_bits(chipwide))

    def ident(c):
        rid, pid, _ = topo.addr(c)
        return DstId(rid=rid, pnc=pid)

    def codes(s, k=1, buf="qx"):
        return T[buf][:, NC * s:NC * (s + k)].bitcast(dt.uint8)

    def planes(s, k=1, buf="sx"):
        return T[buf][:, NC * s:NC * (s + k)]

    g.sync.dma_start(T.bx[:], T.x[:]).then_inc(S.lx, 16)
    g.sync.dma_start(T.ba[:], T.a[:]).then_inc(S.la, 16)
    g.sync.dma_start(T.bw[:, 0:512], T.w[:]).then_inc(S.lw, 16)
    g.sync.dma_start(T.bw[:, 512:1024], T.bb[:]).then_inc(S.lw, 16)

    sent = [0]

    def spread(view, steps, sem):
        g.remote_dma_fused([RemoteDMATransfer(dst_ids=[ident(dsts[k]) for k in steps], dma_engine_mask=link,
                                              remote_sem=sem, srcs=[view(mine)], dsts=[view(2 + k) for k in steps])],
                           local_sem=S.sent)
        sent[0] += NL

    def hand(dst, src, sem, mask):
        rid, pid, _ = topo.addr(mate)
        g.remote_dma(dst, src, sem, S.sent, pid, rid, mask)
        sent[0] += len(_bits(mask))

    g.wait_ge(S.xq, 1)
    for steps, sem in (((0, 1), S.sd0), ((2, 3), S.sd1)):
        spread(planes, steps, sem)
        spread(codes, steps, S["c%d" % rank])
    hand(planes(mine), planes(mine), S.own, inner)
    hand(codes(mine), codes(mine), S.own, inner)
    g.wait_ge(S.sd0, 2 * NL)
    hand(planes(6, 2), planes(2, 2), S.fp0, inner)
    g.wait_ge(S[arr[0]], NL)
    g.wait_ge(S[arr[1]], NL)
    hand(codes(6, 2), codes(2, 2), S.fa, inner)
    g.wait_ge(S.sd1, 2 * NL)
    hand(planes(8, 2), planes(4, 2), S.fp1, inner)
    g.wait_ge(S[arr[2]], NL)
    hand(codes(8), codes(4), S.f2, inner)
    g.wait_ge(S[arr[3]], NL)
    hand(codes(9), codes(5), S.f3, chipwide)
    for to, k in GIVEN:
        (s0, m), d0 = GR[k], GR[to][0]
        g.wait_ge(S["q" + k], 1)
        hand(planes(d0, m, "st"), planes(s0, m, "st"), S["t" + to], chipwide)
        hand(codes(d0, m, "qt"), codes(s0, m, "qt"), S["t" + to], chipwide)
    g.wait_ge(S.sent, sent[0])

    need = {"O": [(S.xq, 1)],
            "P": [(S.own, 2 * NI)],
            "A": [(S.sd0, 2 * NL), (S[arr[0]], NL), (S[arr[1]], NL)],
            "F": [(S.sd1, 2 * NL), (S[arr[2]], NL)],
            "G": [(S.sd1, 2 * NL), (S[arr[3]], NL)],
            "C": [(S.fp0, NI), (S.fa, NI)],
            "D": [(S.fp1, NI), (S.f2, NI)],
            "E": [(S.fp1, NI), (S.f3, NA)]}

    def cols(k):
        return slice(NC * grp[k][0], NC * (grp[k][0] + grp[k][1]))

    def zbank(k, b):
        return T.z[:, 512 * b:512 * b + NC * grp[k][1]]

    def ybank(k):
        return T.yp[:, 512 * YBANK[k]:512 * YBANK[k] + NC * grp[k][1]]

    seen = []
    for op in TENSOR:
        k = op[1]
        if op[0] in "ZW" and k not in seen:
            if not seen:
                g.tensor.wait_ge(S.aq, 1)
            seen.append(k)
            for sem, v in need[k]:
                g.tensor.wait_ge(sem, v)
        if op[0] == "Z":
            i = MADE.index(k)
            for b in range(4):
                if i:
                    g.tensor.wait_ge(S.vs if b % 2 else S.ss, 2 * (i - 1) + b // 2 + 1)
                g.tensor.matmul_mx(zbank(k, b), T.qa[:, NC * b:NC * b + NC], T.sa[:, NC * b:NC * b + NC],
                                   T.qx[:, cols(k)], T.sx[:, cols(k)], True, True).then_inc(S.zs, 1)
        elif op[0] == "W":
            if len(seen) == 1:
                g.tensor.wait_ge(S.wq, 1)
            if k in BEFORE:
                g.tensor.wait_ge(S["e" + BEFORE[k]], 1)
            g.tensor.matmul_mx(ybank(k), T.qw[:, 0:128], T.sw[:, 0:128], T.qx[:, cols(k)], T.sx[:, cols(k)], True, False)
        else:
            if k in MADE:
                g.tensor.wait_ge(S["q" + k], 1)
            else:
                g.tensor.wait_ge(S["t" + k], 2 * NA)
            g.tensor.matmul_mx(ybank(k), T.qw[:, 128:256], T.sw[:, 128:256], T.qt[:, cols(k)], T.st[:, cols(k)],
                               False, True).then_inc(S["y" + k], 1)

    g.vector.wait_ge(S.lx, 16)
    g.vector.quantize_mx(T.qx[:, cols("O")], T.sx[:, cols("O")], T.bx[:]).then_inc(S.xq, 1)
    g.vector.wait_ge(S.la, 16)
    g.vector.quantize_mx(T.qa[:], T.sa[:], T.ba[:]).then_inc(S.aq, 1)
    g.vector.wait_ge(S.lw, 32)
    g.vector.quantize_mx(T.qw[:], T.sw[:], T.bw[:]).then_inc(S.wq, 1)
    for queue, ops in (("s", SCALAR), ("v", VECTOR)):
        e = g.scalar if queue == "s" else g.vector
        for op in ops:
            k = op[1]
            lo, hi = 4 * NC * grp[k][0], 4 * NC * (grp[k][0] + grp[k][1])
            if op[0] == "S":
                i = MADE.index(k)
                for b in ((0, 2) if queue == "s" else (1, 3)):
                    e.wait_ge(S.zs, 4 * i + b + 1)
                    dst, src = T.h[:, lo + b:hi:4], zbank(k, b)
                    if queue == "s":
                        e.activation(dst, src, ActivationFunctionType.Copy, scale=C).then_inc(S.ss, 1)
                    else:
                        e.tensor_scalar(dst, src, C, None, AluOpType.mult).then_inc(S.vs, 1)
            elif op[0] == "Q":
                i = MADE.index(k)
                e.wait_ge(S.vs, 2 * i + 2)
                e.wait_ge(S.ss, 2 * i + 2)
                e.quantize_mx(T.qt[:, cols(k)], T.st[:, cols(k)], T.h[:, lo:hi]).then_inc(S["q" + k], 1)
            else:
                e.wait_ge(S["y" + k], 1)
                if queue == "s":
                    e.activation(T.ys[:, cols(k)], ybank(k), ActivationFunctionType.Copy).then_inc(S["e" + k], 1)
                else:
                    e.tensor_copy(T.ys[:, cols(k)], ybank(k)).then_inc(S["e" + k], 1)

    for k in STORE:
        g.sync.wait_ge(S["e" + k], 1)
        for s in range(grp[k][0], grp[k][0] + grp[k][1]):
            j = slot_rank[s]
            g.sync.dma_start(T.y[:, NC * j:NC * j + NC], T.ys[:, NC * s:NC * s + NC]).then_inc(S.stored, 16)
    g.sync.wait_ge(S.stored, 16 * SLOTS)
